import numpy as np
import ml_dtypes


def mxq(x, axis, fmt="e4m3"):
    dtype, down = {"e4m3": (ml_dtypes.float8_e4m3fn, 7), "e5m2": (ml_dtypes.float8_e5m2, 14)}[fmt]
    v = np.moveaxis(np.asarray(x, np.float32).astype(ml_dtypes.bfloat16).astype(np.float64), axis, -1)
    blocks = v.reshape(v.shape[:-1] + (-1, 32))
    amax = np.abs(blocks).max(-1, keepdims=True)
    byte = np.maximum(np.where(amax > 0, np.frexp(amax)[1] - 1 + 127, 0) - down, 1)
    scale = np.exp2(byte - 127.0)
    codes = (blocks / scale).astype(np.float32).astype(dtype).astype(np.float64)
    return np.moveaxis((codes * scale).reshape(v.shape), -1, axis)


WIDE = False


def mx_kscale(k):
    if not WIDE:
        return np.ones(k)
    levels = np.array([10, -10, 5, -5, 0])
    if k % 512:
        return np.exp2(np.random.permutation(np.resize(levels, k // 32))).repeat(32)
    a = np.empty((k // 512, 16))
    for p in range(k // 512):
        a[p, :8] = np.random.permutation(np.resize(levels, 8))
        for g in range(8):
            far = levels[np.abs(levels - a[p, g]) >= 10]
            a[p, g + 8] = far[np.random.randint(len(far))]
    return np.exp2(a.ravel()).repeat(32)


def f64(x):
    return np.asarray(x).astype(np.float64)


def striped(idx):
    return np.tile(idx.reshape(-1, 16).T, (8, 1)).astype(np.uint16)


def unstriped(offs):
    return offs[:16].T.reshape(-1).astype(np.int64)


def pack_weight(w):
    k, n = w.shape
    w = f64(np.asarray(w, np.float32).astype(ml_dtypes.bfloat16)).reshape(k // 32, 32, n)
    amax = np.abs(w).max(1)
    byte = np.clip(np.where(amax > 0, np.frexp(amax)[1] - 1 + 127 - 7, 1), 1, 254)
    scaled = (w * np.exp2(127.0 - byte)[:, None, :]).reshape(k, n).astype(np.float32)
    words = np.ascontiguousarray(scaled.reshape(k // 512, 128, 4, n).transpose(0, 1, 3, 2)).astype(ml_dtypes.float8_e4m3fn).view(np.uint8)
    return words, np.ascontiguousarray(byte.astype(np.uint8).reshape(k // 512, 16, n))


def unpack_weight(words, scales):
    g, p, n, _ = words.shape
    vals = np.ascontiguousarray(words).view(ml_dtypes.float8_e4m3fn).astype(np.float64) * np.repeat(np.exp2(scales.astype(np.float64) - 127.0), 8, axis=1)[..., None]
    return vals.transpose(0, 1, 3, 2).reshape(g * 512, n)


E2M1 = np.array([0.0, 0.5, 1.0, 1.5, 2.0, 3.0, 4.0, 6.0, -0.0, -0.5, -1.0, -1.5, -2.0, -3.0, -4.0, -6.0])


def pack_fp4(w):
    k, n = w.shape
    w = f64(np.asarray(w, np.float32).astype(ml_dtypes.bfloat16)).reshape(k // 32, 32, n)
    amax = np.abs(w).max(1)
    mant, ex = np.frexp(amax / 6.0)
    byte = np.clip(np.where(amax > 0, np.where(mant > 0.5, ex, ex - 1) + 127, 1), 1, 254)
    scaled = (w * np.exp2(127.0 - byte)[:, None, :]).reshape(k, n).astype(np.float32)
    c = np.ascontiguousarray(scaled.reshape(k // 512, 128, 4, n).transpose(0, 1, 3, 2)).astype(ml_dtypes.float4_e2m1fn).view(np.uint8) & 0xF
    words = (c[..., 0::2] | (c[..., 1::2] << 4)).reshape(k // 512, 128, 2 * n)
    return np.ascontiguousarray(words), np.ascontiguousarray(byte.astype(np.uint8).reshape(k // 512, 16, n))


def unpack_fp4(words, scales):
    g, _, n = scales.shape
    words = np.ascontiguousarray(words).reshape(g, 128, n, 2)
    nib = np.empty((g, 128, n, 4), np.uint8)
    nib[..., 0::2] = words & 0xF
    nib[..., 1::2] = words >> 4
    vals = E2M1[nib] * np.repeat(np.exp2(scales.astype(np.float64) - 127.0), 8, axis=1)[..., None]
    return vals.transpose(0, 1, 3, 2).reshape(g * 512, n)


def relu(v):
    return np.maximum(v, 0.0)


K, T, H, N = 512, 1024, 512, 128


def setup_inputs():
    n = np.random.standard_normal
    s = mx_kscale(K)[:, None]
    u = mx_kscale(H)
    packed_xT = pack_weight(n((K, T)) * s)
    packed_w2 = pack_fp4(n((H, N)) / np.sqrt(2 * H) / u[:, None])
    packed_w3 = pack_fp4(n((H, N)) / np.sqrt(2 * H) / u[:, None])
    return {
        "x_words": packed_xT[0],
        "x_scales": packed_xT[1],
        "w1": (n((K, H)) / np.sqrt(K) / s * u).astype(np.float32),
        "w2_words": packed_w2[0],
        "w2_scales": packed_w2[1],
        "w3_words": packed_w3[0],
        "w3_scales": packed_w3[1],
        "pos1": striped(np.random.permutation(T)),
        "pos2": striped(np.random.permutation(T)),
        "pos3": striped(np.random.permutation(T)),
        "pos4": striped(np.random.permutation(T)),
    }


def reference(x_words, x_scales, w1, w2_words, w2_scales, w3_words, w3_scales, pos1, pos2, pos3, pos4):
    xq = unpack_weight(x_words, x_scales)
    h = relu(mxq(f64(w1), 0, "e4m3").T @ xq)
    z = np.maximum(np.maximum(np.maximum(h[:, unstriped(pos1)], h[:, unstriped(pos2)]), h[:, unstriped(pos3)]), h[:, unstriped(pos4)])
    return unpack_fp4(w2_words, w2_scales).T @ mxq(h, 0, "e4m3") + unpack_fp4(w3_words, w3_scales).T @ mxq(z, 0, "e4m3")

@@ -1,0 +1,193 @@
+from contextlib import ExitStack
+
+import concourse.mybir as mybir
+
+K, T, H, N = 512, 1024, 512, 128
+FLOPS = 2 * K * H * T + 2 * 2 * H * N * T
+
+F32 = mybir.dt.float32
+BF16 = mybir.dt.bfloat16
+I32 = mybir.dt.int32
+U32 = mybir.dt.uint32
+U16 = mybir.dt.uint16
+U8 = mybir.dt.uint8
+FP8X4 = mybir.dt.float8_e4m3fn_x4
+FP4X4 = mybir.dt.float4_e2m1fn_x4
+ACT = mybir.ActivationFunctionType
+ALU = mybir.AluOpType
+
+P = 128
+PACK = 4
+HALF = T // 2
+LISTS = 4
+
+
+def weave_views(dst, src):
+    return (
+        dst.rearrange("p (c i t) -> p c t i", i=4, t=PACK),
+        src.rearrange("p t (c i) -> p c t i", i=4),
+    )
+
+
+def tile_picked_wsagecat_max_l_kernel(
+    tc, x_words, x_scales, w1, w2_words, w2_scales, w3_words, w3_scales, pos1, pos2, pos3, pos4, out
+):
+    nc = tc.nc
+    with ExitStack() as ctx:
+        keep = ctx.enter_context(tc.tile_pool(name="keep", bufs=1))
+        ring = ctx.enter_context(tc.tile_pool(name="ring", bufs=2))
+        psum_h = ctx.enter_context(tc.psum_pool(name="psum_h", bufs=4))
+        psum_o = ctx.enter_context(tc.psum_pool(name="psum_o", bufs=1))
+
+        lists = [keep.tile([P, T // 16], U16, name="list%d" % d) for d in range(LISTS)]
+        x_plane = keep.tile([P, T], U8, name="x_plane", align_bytes=64)
+        w23_plane = keep.tile([P, 2 * N], U8, name="w23_plane", align_bytes=64)
+        w1_raw = [keep.tile([P, PACK, H // 2], F32, name="w1_raw%d" % u) for u in range(2)]
+        x_codes = [keep.tile([P, HALF], U32, name="x_codes%d" % u, align_bytes=64) for u in range(2)]
+        w23_codes = [keep.tile([P, 2 * N], U8, name="w23_codes%d" % u, align_bytes=64) for u in range(2)]
+
+        nc.vector.memset(x_plane[:].bitcast(I32), 0)
+        nc.vector.memset(w23_plane[:].bitcast(I32), 0)
+        w1_rows = w1.rearrange("(p j) c -> p j c", j=PACK)
+        x_flat = x_words[0].rearrange("p n t -> p (n t)").bitcast(I32)
+        nc.sync.dma_start(w1_raw[0][:], w1_rows[:, :, 0 : H // 2])
+        for q in range(4):
+            nc.sync.dma_start(
+                x_plane[32 * q : 32 * q + 4, :].bitcast(I32), x_scales[0][4 * q : 4 * q + 4, :].bitcast(I32)
+            )
+        nc.sync.dma_start(w1_raw[1][:], w1_rows[:, :, H // 2 : H])
+        for u in range(2):
+            nc.sync.dma_start(x_codes[u][:].bitcast(I32), x_flat[:, u * HALF : (u + 1) * HALF])
+        for tile, pos in zip(lists, (pos1, pos2, pos3, pos4)):
+            nc.sync.dma_start(tile[:], pos)
+        for u, (words, scales) in enumerate(((w2_words, w2_scales), (w3_words, w3_scales))):
+            nc.sync.dma_start(w23_codes[u][:].bitcast(I32), words[0].bitcast(I32))
+            for q in range(4):
+                nc.sync.dma_start(
+                    w23_plane[32 * q : 32 * q + 4, u * N : (u + 1) * N].bitcast(I32),
+                    scales[0][4 * q : 4 * q + 4, :].bitcast(I32),
+                )
+
+        w_first = keep.tile([P, P * PACK], BF16, name="w_first", align_bytes=64)
+        w_rest = keep.tile([P, PACK - 1, P * PACK], BF16, name="w_rest", align_bytes=64)
+        w_codes0 = keep.tile([P, P], U32, name="w_codes0", align_bytes=64)
+        w_plane0 = keep.tile([P, P], U8, name="w_plane0", align_bytes=64)
+        w_codes1 = keep.tile([P, P], U32, name="w_codes1", align_bytes=64)
+        w_plane1 = keep.tile([P, P], U8, name="w_plane1", align_bytes=64)
+        w_codes23 = keep.tile([P, 2 * P], U32, name="w_codes23", align_bytes=64)
+        w_plane23 = keep.tile([P, 2 * P], U8, name="w_plane23", align_bytes=64)
+        for u in range(2):
+            dealt = w1_raw[u][:].rearrange("p j (m t) -> p m j t", t=PACK)
+            cols = slice(u * 256, (u + 1) * 256)
+            nc.vector.tensor_copy(w_first[:, cols].rearrange("p (m j) -> p m j", j=PACK), dealt[:, :, :, 0])
+            nc.scalar.activation(
+                w_rest[:, :, cols].rearrange("p t (m j) -> p m j t", j=PACK), dealt[:, :, :, 1:PACK], ACT.Copy
+            )
+        nc.vector.quantize_mx(out=w_codes0[:].bitcast(FP8X4), scales=w_plane0[:], in_=w_first[:])
+        nc.vector.quantize_mx(out=w_codes1[:].bitcast(FP8X4), scales=w_plane1[:], in_=w_rest[:, 0, :])
+        nc.vector.quantize_mx(
+            out=w_codes23[:].bitcast(FP8X4),
+            scales=w_plane23[:],
+            in_=w_rest[:, 1:3, :].rearrange("p t c -> p (t c)"),
+        )
+        stationary = [
+            (w_codes0[:], w_plane0[:]),
+            (w_codes1[:], w_plane1[:]),
+            (w_codes23[:, 0:P], w_plane23[:, 0:P]),
+            (w_codes23[:, P : 2 * P], w_plane23[:, P : 2 * P]),
+        ]
+
+        h = keep.tile([P, PACK * T], F32, name="h")
+        for t in range(PACK):
+            width = 256 if t == 0 else 512
+            for n0 in range(0, T, width):
+                acc = psum_h.tile([P, 512], F32, name="acc")
+                u, c0 = divmod(n0, HALF)
+                nc.tensor.matmul_mx(
+                    out=acc[:, 0:width],
+                    lhsT=stationary[t][0].bitcast(FP8X4),
+                    lhsT_scale=stationary[t][1],
+                    rhs=x_codes[u][:, c0 : c0 + width].bitcast(FP8X4),
+                    rhs_scale=x_plane[:, n0 : n0 + width],
+                    start=True,
+                    stop=True,
+                )
+                dst = h[:, t * T + n0 : t * T + n0 + width]
+                if t == 0 and (n0 // width) % 2 == 1:
+                    nc.vector.tensor_scalar_max(dst, acc[:, 0:width], 0.0)
+                else:
+                    nc.scalar.activation(dst, acc[:, 0:width], ACT.Relu)
+
+        h_woven = keep.tile([P, PACK * T], BF16, name="h_woven", align_bytes=64)
+        h_codes = keep.tile([P, T], U32, name="h_codes", align_bytes=64)
+        h_plane = keep.tile([P, T], U8, name="h_plane", align_bytes=64)
+        h_rows = h[:].rearrange("p (t n) -> p t n", t=PACK)
+        z_rows = keep.tile([P, 2, PACK, HALF], BF16, name="z_rows")
+        z_woven = keep.tile([P, PACK * HALF], BF16, name="z_woven", align_bytes=64)
+        early = keep.tile([P, 2 * LISTS * T], BF16, name="early")
+
+        def largest(t, n0, n, space):
+            fetched = space.rearrange("p (c d r) -> p c d r", c=2, d=LISTS)
+            span = T if n < T else 2 * T
+            window = h[:, t * T : t * T + span]
+            for d in range(LISTS):
+                nc.vector.tensor_copy(fetched[:, :, d, :], window.indirect(lists[d][:, n0 // 16 : (n0 + n) // 16]))
+            pairs = ring.tile([P, 2, 2, n // 2], BF16, name="pairs")
+            nc.vector.tensor_tensor(pairs[:], fetched[:, :, 0:2, :], fetched[:, :, 2:4, :], ALU.max)
+            if n == T:
+                dst = z_rows[:, :, t, :]
+            else:
+                u, c0 = divmod(n0, HALF)
+                dst = z_rows[:, u, t, c0 : c0 + n].rearrange("p (c r) -> p c r", c=2)
+            nc.vector.tensor_tensor(dst, pairs[:, :, 0, :], pairs[:, :, 1, :], ALU.max)
+
+        def finish(n0, n, woven, on_vector):
+            u, c0 = divmod(n0, HALF)
+            dst, src = weave_views(woven, z_rows[:, u, :, c0 : c0 + n])
+            if on_vector:
+                nc.vector.tensor_copy(dst, src)
+            else:
+                nc.scalar.copy(dst, src)
+            z_codes = keep.tile([P, n], U32, name="z_codes%d" % n0, align_bytes=64)
+            z_plane = keep.tile([P, n], U8, name="z_plane%d" % n0, align_bytes=64)
+            nc.vector.quantize_mx(out=z_codes[:].bitcast(FP8X4), scales=z_plane[:], in_=woven)
+            total = psum_o.tile([P, n], F32, name="total%d" % n0)
+            width = 512 if n == 512 else 128
+            for g0 in range(0, n, width):
+                for u2, (codes, plane) in enumerate(
+                    (
+                        (h_codes[:, n0 + g0 : n0 + g0 + width], h_plane[:, n0 + g0 : n0 + g0 + width]),
+                        (z_codes[:, g0 : g0 + width], z_plane[:, g0 : g0 + width]),
+                    )
+                ):
+                    nc.tensor.matmul_mx(
+                        out=total[:, g0 : g0 + width],
+                        lhsT=w23_codes[u2][:].bitcast(FP4X4),
+                        lhsT_scale=w23_plane[:, u2 * N : (u2 + 1) * N],
+                        rhs=codes.bitcast(FP8X4),
+                        rhs_scale=plane,
+                        start=(u2 == 0),
+                        stop=(u2 == 1),
+                    )
+            result = keep.tile([P, n], F32, name="result%d" % n0)
+            nc.scalar.copy(result[:], total[:])
+            nc.sync.dma_start(out[:, n0 : n0 + n], result[:])
+
+        largest(0, 0, HALF, early[:, 0:2048])
+        largest(0, HALF, HALF, early[:, 2048:4096])
+        for u in range(2):
+            dst, src = weave_views(
+                h_woven[:, u * 2048 : (u + 1) * 2048], h_rows[:, :, u * HALF : (u + 1) * HALF]
+            )
+            nc.scalar.activation(dst, src, ACT.Copy)
+        largest(1, 0, T, early[:, 4096:8192])
+        nc.vector.quantize_mx(out=h_codes[:].bitcast(FP8X4), scales=h_plane[:], in_=h_woven[:])
+        largest(2, 0, HALF, h_woven[:, 0:2048])
+        largest(3, 0, HALF, h_woven[:, 2048:4096])
+        finish(0, HALF, z_woven[:], False)
+        largest(2, HALF, HALF, h_woven[:, 0:2048])
+        tail_woven = keep.tile([P, PACK * HALF], BF16, name="tail_woven", align_bytes=64)
+        for n0, n in ((512, 256), (768, 128), (896, 128)):
+            cols = slice(4 * (n0 - HALF), 4 * (n0 - HALF + n))
+            largest(3, n0, n, z_woven[:, cols])
+            finish(n0, n, tail_woven[:, cols], n0 + n == T)

@@ -1,6 +1,7 @@
 from contextlib import ExitStack
 
 import concourse.mybir as mybir
+from concourse.masks import make_identity
 
 K, T, H, N = 512, 1024, 512, 128
 FLOPS = 2 * K * H * T + 2 * 2 * H * N * T
@@ -20,6 +21,7 @@ P = 128
 PACK = 4
 HALF = T // 2
 LISTS = 4
+TURNED = 768
 
 
 def weave_views(dst, src):
@@ -35,14 +37,13 @@ def tile_picked_wsagecat_max_l_kernel(
     nc = tc.nc
     with ExitStack() as ctx:
         keep = ctx.enter_context(tc.tile_pool(name="keep", bufs=1))
-        ring = ctx.enter_context(tc.tile_pool(name="ring", bufs=2))
-        psum_h = ctx.enter_context(tc.psum_pool(name="psum_h", bufs=4))
-        psum_o = ctx.enter_context(tc.psum_pool(name="psum_o", bufs=1))
+        psum = ctx.enter_context(tc.psum_pool(name="psum", bufs=1))
+        banks = [psum.tile([P, 512], F32, name="bank%d" % b) for b in range(8)]
 
         lists = [keep.tile([P, T // 16], U16, name="list%d" % d) for d in range(LISTS)]
         x_plane = keep.tile([P, T], U8, name="x_plane", align_bytes=64)
         w23_plane = keep.tile([P, 2 * N], U8, name="w23_plane", align_bytes=64)
-        w1_raw = [keep.tile([P, PACK, H // 2], F32, name="w1_raw%d" % u) for u in range(2)]
+        w1_raw = [keep.tile([P, 2, H], F32, name="w1_raw%d" % u) for u in range(2)]
         x_codes = [keep.tile([P, HALF], U32, name="x_codes%d" % u, align_bytes=64) for u in range(2)]
         w23_codes = [keep.tile([P, 2 * N], U8, name="w23_codes%d" % u, align_bytes=64) for u in range(2)]
 
@@ -50,12 +51,12 @@ def tile_picked_wsagecat_max_l_kernel(
         nc.vector.memset(w23_plane[:].bitcast(I32), 0)
         w1_rows = w1.rearrange("(p j) c -> p j c", j=PACK)
         x_flat = x_words[0].rearrange("p n t -> p (n t)").bitcast(I32)
-        nc.sync.dma_start(w1_raw[0][:], w1_rows[:, :, 0 : H // 2])
+        nc.sync.dma_start(w1_raw[0][:], w1_rows[:, 0:2, :])
+        nc.sync.dma_start(w1_raw[1][:], w1_rows[:, 2:4, :])
         for q in range(4):
             nc.sync.dma_start(
                 x_plane[32 * q : 32 * q + 4, :].bitcast(I32), x_scales[0][4 * q : 4 * q + 4, :].bitcast(I32)
             )
-        nc.sync.dma_start(w1_raw[1][:], w1_rows[:, :, H // 2 : H])
         for u in range(2):
             nc.sync.dma_start(x_codes[u][:].bitcast(I32), x_flat[:, u * HALF : (u + 1) * HALF])
         for tile, pos in zip(lists, (pos1, pos2, pos3, pos4)):
@@ -78,10 +79,10 @@ def tile_picked_wsagecat_max_l_kernel(
         w_plane23 = keep.tile([P, 2 * P], U8, name="w_plane23", align_bytes=64)
         for u in range(2):
             dealt = w1_raw[u][:].rearrange("p j (m t) -> p m j t", t=PACK)
-            cols = slice(u * 256, (u + 1) * 256)
-            nc.vector.tensor_copy(w_first[:, cols].rearrange("p (m j) -> p m j", j=PACK), dealt[:, :, :, 0])
+            rows = slice(2 * u, 2 * u + 2)
+            nc.vector.tensor_copy(w_first[:].rearrange("p (m j) -> p m j", j=PACK)[:, :, rows], dealt[:, :, :, 0])
             nc.scalar.activation(
-                w_rest[:, :, cols].rearrange("p t (m j) -> p m j t", j=PACK), dealt[:, :, :, 1:PACK], ACT.Copy
+                w_rest[:].rearrange("p t (m j) -> p m j t", j=PACK)[:, :, rows, :], dealt[:, :, :, 1:PACK], ACT.Copy
             )
         nc.vector.quantize_mx(out=w_codes0[:].bitcast(FP8X4), scales=w_plane0[:], in_=w_first[:])
         nc.vector.quantize_mx(out=w_codes1[:].bitcast(FP8X4), scales=w_plane1[:], in_=w_rest[:, 0, :])
@@ -97,11 +98,16 @@ def tile_picked_wsagecat_max_l_kernel(
             (w_codes23[:, P : 2 * P], w_plane23[:, P : 2 * P]),
         ]
 
-        h = keep.tile([P, PACK * T], F32, name="h")
+        ident = keep.tile([P, P], F32, name="ident")
+        make_identity(nc, ident[:])
+        h = [keep.tile([P, T], F32, name="h%d" % t) for t in range(PACK)]
+        h_rows = keep.tile([P, PACK, T], F32, name="h_rows")
+        turn = 0
         for t in range(PACK):
             width = 256 if t == 0 else 512
             for n0 in range(0, T, width):
-                acc = psum_h.tile([P, 512], F32, name="acc")
+                acc = banks[turn % 8]
+                turn = turn + 1
                 u, c0 = divmod(n0, HALF)
                 nc.tensor.matmul_mx(
                     out=acc[:, 0:width],
@@ -112,46 +118,73 @@ def tile_picked_wsagecat_max_l_kernel(
                     start=True,
                     stop=True,
                 )
-                dst = h[:, t * T + n0 : t * T + n0 + width]
-                if t == 0 and (n0 // width) % 2 == 1:
+                dst = h[t][:, n0 : n0 + width]
+                if t == 0 and n0 + width == T:
                     nc.vector.tensor_scalar_max(dst, acc[:, 0:width], 0.0)
                 else:
                     nc.scalar.activation(dst, acc[:, 0:width], ACT.Relu)
+            nc.sync.dma_start(h_rows[:, t, :], h[t][:])
 
         h_woven = keep.tile([P, PACK * T], BF16, name="h_woven", align_bytes=64)
         h_codes = keep.tile([P, T], U32, name="h_codes", align_bytes=64)
         h_plane = keep.tile([P, T], U8, name="h_plane", align_bytes=64)
-        h_rows = h[:].rearrange("p (t n) -> p t n", t=PACK)
-        z_rows = keep.tile([P, 2, PACK, HALF], BF16, name="z_rows")
-        z_woven = keep.tile([P, PACK * HALF], BF16, name="z_woven", align_bytes=64)
-        early = keep.tile([P, 2 * LISTS * T], BF16, name="early")
 
-        def largest(t, n0, n, space):
-            fetched = space.rearrange("p (c d r) -> p c d r", c=2, d=LISTS)
-            span = T if n < T else 2 * T
-            window = h[:, t * T : t * T + span]
-            for d in range(LISTS):
-                nc.vector.tensor_copy(fetched[:, :, d, :], window.indirect(lists[d][:, n0 // 16 : (n0 + n) // 16]))
-            pairs = ring.tile([P, 2, 2, n // 2], BF16, name="pairs")
-            nc.vector.tensor_tensor(pairs[:], fetched[:, :, 0:2, :], fetched[:, :, 2:4, :], ALU.max)
-            if n == T:
-                dst = z_rows[:, :, t, :]
-            else:
-                u, c0 = divmod(n0, HALF)
-                dst = z_rows[:, u, t, c0 : c0 + n].rearrange("p (c r) -> p c r", c=2)
-            nc.vector.tensor_tensor(dst, pairs[:, :, 0, :], pairs[:, :, 1, :], ALU.max)
+        def looked_up(t, d, n0, n):
+            return h[t][:].indirect(lists[d][:, n0 // 16 : (n0 + n) // 16])
 
-        def finish(n0, n, woven, on_vector):
-            u, c0 = divmod(n0, HALF)
-            dst, src = weave_views(woven, z_rows[:, u, :, c0 : c0 + n])
-            if on_vector:
-                nc.vector.tensor_copy(dst, src)
-            else:
-                nc.scalar.copy(dst, src)
+        def fetch_pairs(t, n0, n, firsts, diffs):
+            for k in range(2):
+                nc.vector.tensor_copy(firsts[k], looked_up(t, 2 * k, n0, n))
+            for k in range(2):
+                nc.vector.tensor_tensor(diffs[k], looked_up(t, 2 * k + 1, n0, n), firsts[k], ALU.subtract)
+
+        def pairs_with_gains(t, n0, n, firsts, diffs, gains):
+            fetch_pairs(t, n0, n, firsts, diffs)
+            for k in range(2):
+                nc.scalar.activation(gains[k], diffs[k], ACT.Relu)
+            return [(firsts[k], gains[k]) for k in range(2)]
+
+        def fresh(label, n):
+            return [keep.tile([P, n], F32, name="%s%d" % (label, k))[:] for k in range(2)]
+
+        def turned_sums(two, n, larger, first_bank):
+            for k in range(2):
+                for c0 in range(0, n, 256):
+                    bank = banks[(first_bank + (k * n + c0) // 256) % 8]
+                    for e in range(2):
+                        for b in range(2):
+                            cols = slice(c0 + b * P, c0 + (b + 1) * P)
+                            spot = bank[:, (2 * b + e) * P : (2 * b + e + 1) * P]
+                            first, gain = two[e][k]
+                            nc.tensor.matmul(spot, first[:, cols], ident[:], start=True, stop=False, is_transpose=True)
+                            nc.tensor.matmul(spot, gain[:, cols], ident[:], start=False, stop=True, is_transpose=True)
+                    nc.scalar.copy(
+                        larger[k][:, 2 * c0 : 2 * c0 + 512].rearrange("q (b p e) -> q b p e", b=2, e=2),
+                        bank[:].rearrange("q (b e p) -> q b p e", b=2, e=2),
+                    )
+
+        def turn_back(n0, woven, bank, halves):
+            for b in range(2):
+                for u in range(halves):
+                    col = n0 + b * P
+                    nc.tensor.transpose(
+                        bank[:, (2 * b + u) * P : (2 * b + u + 1) * P],
+                        z_turned[u][:, 2 * col : 2 * col + 2 * P].bitcast(F32),
+                        ident[:],
+                    )
+            nc.scalar.copy(
+                woven.bitcast(F32).rearrange("p (b n u) -> p b n u", b=2, u=2)[:, :, :, 0:halves],
+                bank[:].rearrange("p (b u n) -> p b n u", b=2, u=2)[:, :, :, 0:halves],
+            )
+
+        def quantise(n0, n, woven):
             z_codes = keep.tile([P, n], U32, name="z_codes%d" % n0, align_bytes=64)
             z_plane = keep.tile([P, n], U8, name="z_plane%d" % n0, align_bytes=64)
             nc.vector.quantize_mx(out=z_codes[:].bitcast(FP8X4), scales=z_plane[:], in_=woven)
-            total = psum_o.tile([P, n], F32, name="total%d" % n0)
+            return z_codes, z_plane
+
+        def finish(n0, n, quantised, total):
+            z_codes, z_plane = quantised
             width = 512 if n == 512 else 128
             for g0 in range(0, n, width):
                 for u2, (codes, plane) in enumerate(
@@ -170,24 +203,107 @@ def tile_picked_wsagecat_max_l_kernel(
                         stop=(u2 == 1),
                     )
             result = keep.tile([P, n], F32, name="result%d" % n0)
-            nc.scalar.copy(result[:], total[:])
+            if n0 + n == T:
+                nc.vector.tensor_copy(result[:], total[:, 0:n])
+            else:
+                nc.scalar.copy(result[:], total[:, 0:n])
             nc.sync.dma_start(out[:, n0 : n0 + n], result[:])
 
-        largest(0, 0, HALF, early[:, 0:2048])
-        largest(0, HALF, HALF, early[:, 2048:4096])
-        for u in range(2):
-            dst, src = weave_views(
-                h_woven[:, u * 2048 : (u + 1) * 2048], h_rows[:, :, u * HALF : (u + 1) * HALF]
-            )
-            nc.scalar.activation(dst, src, ACT.Copy)
-        largest(1, 0, T, early[:, 4096:8192])
+        def largest(dst, one, other):
+            nc.vector.tensor_tensor(dst, one, other, ALU.max)
+
+        REST = T - TURNED
+        z_rows = keep.tile([P, 2, REST], BF16, name="z_rows")
+        z_turned = [
+            keep.tile([P, 2 * n], BF16, name="z_turned%d" % u, align_bytes=64) for u, n in enumerate((T, TURNED))
+        ]
+        larger_low = [keep.tile([P, 2 * T], BF16, name="larger_low%d" % k) for k in range(2)]
+        larger_high = [keep.tile([P, 2 * TURNED], BF16, name="larger_high%d" % k) for k in range(2)]
+        woven_a = keep.tile([P, PACK * HALF], BF16, name="woven_a", align_bytes=64)
+        woven_b = keep.tile([P, PACK * 256], BF16, name="woven_b", align_bytes=64)
+        woven_rest = keep.tile([P, PACK * REST], BF16, name="woven_rest", align_bytes=64)
+
+        low_sets = []
+        for t in range(2):
+            firsts = fresh("first%d_" % t, T)
+            diffs = fresh("diff%d_" % t, T)
+            gains = diffs if t == 0 else [h_rows[:, k, :] for k in range(2)]
+            for n0 in range(0, T, HALF):
+                cols = slice(n0, n0 + HALF)
+                pairs_with_gains(
+                    t, n0, HALF, [x[:, cols] for x in firsts], [x[:, cols] for x in diffs], [x[:, cols] for x in gains]
+                )
+            low_sets.append([(firsts[k], gains[k]) for k in range(2)])
+            if t == 0:
+                for u in range(2):
+                    dst, src = weave_views(
+                        h_woven[:, u * 2048 : (u + 1) * 2048], h_rows[:, :, u * HALF : (u + 1) * HALF]
+                    )
+                    nc.scalar.activation(dst, src, ACT.Copy)
         nc.vector.quantize_mx(out=h_codes[:].bitcast(FP8X4), scales=h_plane[:], in_=h_woven[:])
-        largest(2, 0, HALF, h_woven[:, 0:2048])
-        largest(3, 0, HALF, h_woven[:, 2048:4096])
-        finish(0, HALF, z_woven[:], False)
-        largest(2, HALF, HALF, h_woven[:, 0:2048])
-        tail_woven = keep.tile([P, PACK * HALF], BF16, name="tail_woven", align_bytes=64)
-        for n0, n in ((512, 256), (768, 128), (896, 128)):
-            cols = slice(4 * (n0 - HALF), 4 * (n0 - HALF + n))
-            largest(3, n0, n, z_woven[:, cols])
-            finish(n0, n, tail_woven[:, cols], n0 + n == T)
+        turned_sums(low_sets, T, [tile[:] for tile in larger_low], 2)
+        reuse = h_woven[:].bitcast(F32)
+        set2a = pairs_with_gains(
+            2,
+            0,
+            HALF,
+            [reuse[:, k * HALF : (k + 1) * HALF] for k in range(2)],
+            fresh("diff2a_", HALF),
+            [low_sets[1][1][k][:, HALF:T] for k in range(2)],
+        )
+        diff3a = fresh("diff3a_", HALF)
+        set3a = pairs_with_gains(
+            3,
+            0,
+            HALF,
+            [reuse[:, (2 + k) * HALF : (3 + k) * HALF] for k in range(2)],
+            diff3a,
+            fresh("gain3a_", HALF),
+        )
+        largest(z_turned[0][:], larger_low[0][:], larger_low[1][:])
+        turned_sums([set2a, set3a], HALF, [tile[:, 0:1024] for tile in larger_high], 2)
+        turn_back(TURNED, woven_rest[:], banks[6], 1)
+        high_b = []
+        for e in range(2):
+            both = keep.tile([P, HALF], F32, name="diff%db" % (2 + e))
+            halves = [slice(k * 256, (k + 1) * 256) for k in range(2)]
+            firsts = [diff3a[e][:, half] for half in halves]
+            fetch_pairs(2 + e, HALF, 256, firsts, [both[:, half] for half in halves])
+            gains = set3a[1][e]
+            nc.scalar.activation(gains, both[:], ACT.Relu)
+            high_b.append([(firsts[k], gains[:, halves[k]]) for k in range(2)])
+        largest(z_turned[1][:, 0:1024], larger_high[0][:, 0:1024], larger_high[1][:, 0:1024])
+        turned_sums(high_b, 256, [tile[:, 1024:1536] for tile in larger_high], 7)
+
+        space = larger_high[0]
+        for d in range(LISTS):
+            nc.vector.tensor_copy(space[:, d * REST : (d + 1) * REST], looked_up(2, d, TURNED, REST))
+        pairs = keep.tile([P, 2 * REST], BF16, name="pairs")
+        largest(pairs[:], space[:, 0 : 2 * REST], space[:, 2 * REST : 4 * REST])
+        largest(z_rows[:, 0, :], pairs[:, 0:REST], pairs[:, REST : 2 * REST])
+        largest(z_turned[1][:, 1024:1536], larger_high[0][:, 1024:1536], larger_high[1][:, 1024:1536])
+        for c in range(2):
+            turn_back(256 * c, woven_a[:, 1024 * c : 1024 * (c + 1)], banks[1 + c], 2)
+        quantised_a = quantise(0, HALF, woven_a[:])
+        three = [larger_high[0][:, 1024:1280], larger_high[1][:, 1024:1280], woven_a[:, 0:REST]]
+        for d in range(3):
+            nc.vector.tensor_copy(three[d], looked_up(3, d, TURNED, REST))
+        largest(pairs[:, 0:REST], three[0], three[1])
+        largest(pairs[:, REST : 2 * REST], pairs[:, 0:REST], three[2])
+        turn_back(HALF, woven_b[:], banks[3], 2)
+        quantised_b = quantise(HALF, 256, woven_b[:])
+        finish(0, HALF, quantised_a, banks[4])
+        finish(HALF, 256, quantised_b, banks[5])
+        for c in range(2):
+            nc.vector.tensor_copy(woven_b[:, c * P : (c + 1) * P], looked_up(3, 3, TURNED + c * P, P))
+        for c in range(2):
+            cols = slice(c * P, (c + 1) * P)
+            largest(z_rows[:, 1, cols], pairs[:, REST + c * P : REST + (c + 1) * P], woven_b[:, cols])
+        for c in range(2):
+            nc.vector.tensor_copy(
+                woven_rest[:, c * 512 : (c + 1) * 512].rearrange("p (n u e) -> p n u e", u=2, e=2)[:, :, 1, :],
+                z_rows[:, :, c * P : (c + 1) * P].rearrange("p e n -> p n e"),
+            )
+        for c in range(2):
+            n0 = TURNED + c * P
+            finish(n0, P, quantise(n0, P, woven_rest[:, c * 512 : (c + 1) * 512]), banks[6 + c])

@@ -19,16 +19,13 @@ ALU = mybir.AluOpType
 
 P = 128
 PACK = 4
-HALF = T // 2
 LISTS = 4
-TURNED = 768
-
-
-def weave_views(dst, src):
-    return (
-        dst.rearrange("p (c i t) -> p c t i", i=4, t=PACK),
-        src.rearrange("p t (c i) -> p c t i", i=4),
-    )
+BANKS = 8
+BANK = 512
+HALF = T // 2
+UNIT = 256
+TURNED = HALF + UNIT
+REST = T - TURNED
 
 
 def tile_picked_wsagecat_max_l_kernel(
@@ -38,96 +35,95 @@ def tile_picked_wsagecat_max_l_kernel(
     with ExitStack() as ctx:
         keep = ctx.enter_context(tc.tile_pool(name="keep", bufs=1))
         psum = ctx.enter_context(tc.psum_pool(name="psum", bufs=1))
-        banks = [psum.tile([P, 512], F32, name="bank%d" % b) for b in range(8)]
+        banks = [psum.tile([P, BANK], F32, name="bank%d" % number) for number in range(BANKS)]
 
         lists = [keep.tile([P, T // 16], U16, name="list%d" % d) for d in range(LISTS)]
-        x_plane = keep.tile([P, T], U8, name="x_plane", align_bytes=64)
-        w23_plane = keep.tile([P, 2 * N], U8, name="w23_plane", align_bytes=64)
-        w1_raw = [keep.tile([P, 2, H], F32, name="w1_raw%d" % u) for u in range(2)]
-        x_codes = [keep.tile([P, HALF], U32, name="x_codes%d" % u, align_bytes=64) for u in range(2)]
-        w23_codes = [keep.tile([P, 2 * N], U8, name="w23_codes%d" % u, align_bytes=64) for u in range(2)]
+        x_scale = keep.tile([P, T], U8, name="x_scale", align_bytes=64)
+        w23_scale = keep.tile([P, 2 * N], U8, name="w23_scale", align_bytes=64)
+        w1_raw = [keep.tile([P, 2, H], F32, name="w1_raw%d" % half) for half in range(2)]
+        x_codes = [keep.tile([P, HALF], U32, name="x_codes%d" % half, align_bytes=64) for half in range(2)]
+        w23_codes = [keep.tile([P, 2 * N], U8, name="w%d_codes" % w, align_bytes=64) for w in (2, 3)]
 
-        nc.vector.memset(x_plane[:].bitcast(I32), 0)
-        nc.vector.memset(w23_plane[:].bitcast(I32), 0)
+        nc.vector.memset(x_scale[:].bitcast(I32), 0)
+        nc.vector.memset(w23_scale[:].bitcast(I32), 0)
         w1_rows = w1.rearrange("(p j) c -> p j c", j=PACK)
         x_flat = x_words[0].rearrange("p n t -> p (n t)").bitcast(I32)
-        nc.sync.dma_start(w1_raw[0][:], w1_rows[:, 0:2, :])
-        nc.sync.dma_start(w1_raw[1][:], w1_rows[:, 2:4, :])
+        for half in range(2):
+            nc.sync.dma_start(w1_raw[half][:], w1_rows[:, 2 * half : 2 * half + 2, :])
         for q in range(4):
             nc.sync.dma_start(
-                x_plane[32 * q : 32 * q + 4, :].bitcast(I32), x_scales[0][4 * q : 4 * q + 4, :].bitcast(I32)
+                x_scale[32 * q : 32 * q + 4, :].bitcast(I32), x_scales[0][4 * q : 4 * q + 4, :].bitcast(I32)
             )
-        for u in range(2):
-            nc.sync.dma_start(x_codes[u][:].bitcast(I32), x_flat[:, u * HALF : (u + 1) * HALF])
+        for half in range(2):
+            nc.sync.dma_start(x_codes[half][:].bitcast(I32), x_flat[:, half * HALF : (half + 1) * HALF])
         for tile, pos in zip(lists, (pos1, pos2, pos3, pos4)):
             nc.sync.dma_start(tile[:], pos)
-        for u, (words, scales) in enumerate(((w2_words, w2_scales), (w3_words, w3_scales))):
-            nc.sync.dma_start(w23_codes[u][:].bitcast(I32), words[0].bitcast(I32))
+        for which, (words, scales) in enumerate(((w2_words, w2_scales), (w3_words, w3_scales))):
+            nc.sync.dma_start(w23_codes[which][:].bitcast(I32), words[0].bitcast(I32))
             for q in range(4):
                 nc.sync.dma_start(
-                    w23_plane[32 * q : 32 * q + 4, u * N : (u + 1) * N].bitcast(I32),
+                    w23_scale[32 * q : 32 * q + 4, which * N : (which + 1) * N].bitcast(I32),
                     scales[0][4 * q : 4 * q + 4, :].bitcast(I32),
                 )
 
         w_first = keep.tile([P, P * PACK], BF16, name="w_first", align_bytes=64)
-        w_rest = keep.tile([P, PACK - 1, P * PACK], BF16, name="w_rest", align_bytes=64)
+        w_others = keep.tile([P, PACK - 1, P * PACK], BF16, name="w_others", align_bytes=64)
         w_codes0 = keep.tile([P, P], U32, name="w_codes0", align_bytes=64)
-        w_plane0 = keep.tile([P, P], U8, name="w_plane0", align_bytes=64)
+        w_scale0 = keep.tile([P, P], U8, name="w_scale0", align_bytes=64)
         w_codes1 = keep.tile([P, P], U32, name="w_codes1", align_bytes=64)
-        w_plane1 = keep.tile([P, P], U8, name="w_plane1", align_bytes=64)
+        w_scale1 = keep.tile([P, P], U8, name="w_scale1", align_bytes=64)
         w_codes23 = keep.tile([P, 2 * P], U32, name="w_codes23", align_bytes=64)
-        w_plane23 = keep.tile([P, 2 * P], U8, name="w_plane23", align_bytes=64)
-        for u in range(2):
-            dealt = w1_raw[u][:].rearrange("p j (m t) -> p m j t", t=PACK)
-            rows = slice(2 * u, 2 * u + 2)
+        w_scale23 = keep.tile([P, 2 * P], U8, name="w_scale23", align_bytes=64)
+        for half in range(2):
+            dealt = w1_raw[half][:].rearrange("p j (m t) -> p m j t", t=PACK)
+            rows = slice(2 * half, 2 * half + 2)
             nc.vector.tensor_copy(w_first[:].rearrange("p (m j) -> p m j", j=PACK)[:, :, rows], dealt[:, :, :, 0])
             nc.scalar.activation(
-                w_rest[:].rearrange("p t (m j) -> p m j t", j=PACK)[:, :, rows, :], dealt[:, :, :, 1:PACK], ACT.Copy
+                w_others[:].rearrange("p t (m j) -> p m j t", j=PACK)[:, :, rows, :],
+                dealt[:, :, :, 1:PACK],
+                ACT.Copy,
             )
-        nc.vector.quantize_mx(out=w_codes0[:].bitcast(FP8X4), scales=w_plane0[:], in_=w_first[:])
-        nc.vector.quantize_mx(out=w_codes1[:].bitcast(FP8X4), scales=w_plane1[:], in_=w_rest[:, 0, :])
+        nc.vector.quantize_mx(out=w_codes0[:].bitcast(FP8X4), scales=w_scale0[:], in_=w_first[:])
+        nc.vector.quantize_mx(out=w_codes1[:].bitcast(FP8X4), scales=w_scale1[:], in_=w_others[:, 0, :])
         nc.vector.quantize_mx(
             out=w_codes23[:].bitcast(FP8X4),
-            scales=w_plane23[:],
-            in_=w_rest[:, 1:3, :].rearrange("p t c -> p (t c)"),
+            scales=w_scale23[:],
+            in_=w_others[:, 1:3, :].rearrange("p t c -> p (t c)"),
         )
         stationary = [
-            (w_codes0[:], w_plane0[:]),
-            (w_codes1[:], w_plane1[:]),
-            (w_codes23[:, 0:P], w_plane23[:, 0:P]),
-            (w_codes23[:, P : 2 * P], w_plane23[:, P : 2 * P]),
+            (w_codes0[:], w_scale0[:]),
+            (w_codes1[:], w_scale1[:]),
+            (w_codes23[:, 0:P], w_scale23[:, 0:P]),
+            (w_codes23[:, P : 2 * P], w_scale23[:, P : 2 * P]),
         ]
 
         ident = keep.tile([P, P], F32, name="ident")
         make_identity(nc, ident[:])
         h = [keep.tile([P, T], F32, name="h%d" % t) for t in range(PACK)]
         h_rows = keep.tile([P, PACK, T], F32, name="h_rows")
-        turn = 0
         for t in range(PACK):
-            width = 256 if t == 0 else 512
-            for n0 in range(0, T, width):
-                acc = banks[turn % 8]
-                turn = turn + 1
-                u, c0 = divmod(n0, HALF)
+            width = T // 4 if t == 0 else HALF
+            for piece, n0 in enumerate(range(0, T, width)):
+                acc = banks[piece if t == 0 else 2 + piece][:, 0:width]
+                half, c0 = divmod(n0, HALF)
                 nc.tensor.matmul_mx(
-                    out=acc[:, 0:width],
+                    out=acc,
                     lhsT=stationary[t][0].bitcast(FP8X4),
                     lhsT_scale=stationary[t][1],
-                    rhs=x_codes[u][:, c0 : c0 + width].bitcast(FP8X4),
-                    rhs_scale=x_plane[:, n0 : n0 + width],
+                    rhs=x_codes[half][:, c0 : c0 + width].bitcast(FP8X4),
+                    rhs_scale=x_scale[:, n0 : n0 + width],
                     start=True,
                     stop=True,
                 )
-                dst = h[t][:, n0 : n0 + width]
                 if t == 0 and n0 + width == T:
-                    nc.vector.tensor_scalar_max(dst, acc[:, 0:width], 0.0)
+                    nc.vector.tensor_scalar_max(h[t][:, n0 : n0 + width], acc, 0.0)
                 else:
-                    nc.scalar.activation(dst, acc[:, 0:width], ACT.Relu)
+                    nc.scalar.activation(h[t][:, n0 : n0 + width], acc, ACT.Relu)
             nc.sync.dma_start(h_rows[:, t, :], h[t][:])
 
         h_woven = keep.tile([P, PACK * T], BF16, name="h_woven", align_bytes=64)
         h_codes = keep.tile([P, T], U32, name="h_codes", align_bytes=64)
-        h_plane = keep.tile([P, T], U8, name="h_plane", align_bytes=64)
+        h_scale = keep.tile([P, T], U8, name="h_scale", align_bytes=64)
 
         def looked_up(t, d, n0, n):
             return h[t][:].indirect(lists[d][:, n0 // 16 : (n0 + n) // 16])
@@ -144,166 +140,178 @@ def tile_picked_wsagecat_max_l_kernel(
                 nc.scalar.activation(gains[k], diffs[k], ACT.Relu)
             return [(firsts[k], gains[k]) for k in range(2)]
 
-        def fresh(label, n):
+        def two_tiles(label, n):
             return [keep.tile([P, n], F32, name="%s%d" % (label, k))[:] for k in range(2)]
 
-        def turned_sums(two, n, larger, first_bank):
+        def turned_sums(sets, n, larger, first_bank):
             for k in range(2):
-                for c0 in range(0, n, 256):
-                    bank = banks[(first_bank + (k * n + c0) // 256) % 8]
+                for c0 in range(0, n, UNIT):
+                    bank = banks[(first_bank + (k * n + c0) // UNIT) % BANKS]
                     for e in range(2):
                         for b in range(2):
                             cols = slice(c0 + b * P, c0 + (b + 1) * P)
                             spot = bank[:, (2 * b + e) * P : (2 * b + e + 1) * P]
-                            first, gain = two[e][k]
+                            first, gain = sets[e][k]
                             nc.tensor.matmul(spot, first[:, cols], ident[:], start=True, stop=False, is_transpose=True)
                             nc.tensor.matmul(spot, gain[:, cols], ident[:], start=False, stop=True, is_transpose=True)
                     nc.scalar.copy(
-                        larger[k][:, 2 * c0 : 2 * c0 + 512].rearrange("q (b p e) -> q b p e", b=2, e=2),
+                        larger[k][:, 2 * c0 : 2 * (c0 + UNIT)].rearrange("q (b p e) -> q b p e", b=2, e=2),
                         bank[:].rearrange("q (b e p) -> q b p e", b=2, e=2),
                     )
 
-        def turn_back(n0, woven, bank, halves):
+        def turn_back(n0, woven, bank, pairs_of_sets):
             for b in range(2):
-                for u in range(halves):
+                for u in range(pairs_of_sets):
                     col = n0 + b * P
                     nc.tensor.transpose(
                         bank[:, (2 * b + u) * P : (2 * b + u + 1) * P],
-                        z_turned[u][:, 2 * col : 2 * col + 2 * P].bitcast(F32),
+                        z_turned[u][:, 2 * col : 2 * (col + P)].bitcast(F32),
                         ident[:],
                     )
             nc.scalar.copy(
-                woven.bitcast(F32).rearrange("p (b n u) -> p b n u", b=2, u=2)[:, :, :, 0:halves],
-                bank[:].rearrange("p (b u n) -> p b n u", b=2, u=2)[:, :, :, 0:halves],
+                woven.bitcast(F32).rearrange("p (b n u) -> p b n u", b=2, u=2)[:, :, :, 0:pairs_of_sets],
+                bank[:].rearrange("p (b u n) -> p b n u", b=2, u=2)[:, :, :, 0:pairs_of_sets],
             )
 
         def quantise(n0, n, woven):
             z_codes = keep.tile([P, n], U32, name="z_codes%d" % n0, align_bytes=64)
-            z_plane = keep.tile([P, n], U8, name="z_plane%d" % n0, align_bytes=64)
-            nc.vector.quantize_mx(out=z_codes[:].bitcast(FP8X4), scales=z_plane[:], in_=woven)
-            return z_codes, z_plane
+            z_scale = keep.tile([P, n], U8, name="z_scale%d" % n0, align_bytes=64)
+            nc.vector.quantize_mx(out=z_codes[:].bitcast(FP8X4), scales=z_scale[:], in_=woven)
+            return z_codes, z_scale
 
-        def finish(n0, n, quantised, total):
-            z_codes, z_plane = quantised
-            width = 512 if n == 512 else 128
-            for g0 in range(0, n, width):
-                for u2, (codes, plane) in enumerate(
-                    (
-                        (h_codes[:, n0 + g0 : n0 + g0 + width], h_plane[:, n0 + g0 : n0 + g0 + width]),
-                        (z_codes[:, g0 : g0 + width], z_plane[:, g0 : g0 + width]),
-                    )
-                ):
-                    nc.tensor.matmul_mx(
-                        out=total[:, g0 : g0 + width],
-                        lhsT=w23_codes[u2][:].bitcast(FP4X4),
-                        lhsT_scale=w23_plane[:, u2 * N : (u2 + 1) * N],
-                        rhs=codes.bitcast(FP8X4),
-                        rhs_scale=plane,
-                        start=(u2 == 0),
-                        stop=(u2 == 1),
-                    )
-            result = keep.tile([P, n], F32, name="result%d" % n0)
-            if n0 + n == T:
-                nc.vector.tensor_copy(result[:], total[:, 0:n])
-            else:
-                nc.scalar.copy(result[:], total[:, 0:n])
-            nc.sync.dma_start(out[:, n0 : n0 + n], result[:])
+        def second_product(which, codes, scale, total):
+            nc.tensor.matmul_mx(
+                out=total,
+                lhsT=w23_codes[which][:].bitcast(FP4X4),
+                lhsT_scale=w23_scale[:, which * N : (which + 1) * N],
+                rhs=codes.bitcast(FP8X4),
+                rhs_scale=scale,
+                start=(which == 0),
+                stop=(which == 1),
+            )
+
+        def finish(n0, n, quantised, result):
+            z_codes, z_scale = quantised
+            for g0, width, bank in groups:
+                if n0 <= g0 < n0 + n:
+                    cols = slice(g0 - n0, g0 - n0 + width)
+                    second_product(1, z_codes[:, cols], z_scale[:, cols], bank[:, 0:width])
+                    if g0 + width == T:
+                        nc.vector.tensor_copy(result[:, cols], bank[:, 0:width])
+                    else:
+                        nc.scalar.copy(result[:, cols], bank[:, 0:width])
+            nc.sync.dma_start(out[:, n0 : n0 + n], result)
 
         def largest(dst, one, other):
             nc.vector.tensor_tensor(dst, one, other, ALU.max)
 
-        REST = T - TURNED
         z_rows = keep.tile([P, 2, REST], BF16, name="z_rows")
         z_turned = [
             keep.tile([P, 2 * n], BF16, name="z_turned%d" % u, align_bytes=64) for u, n in enumerate((T, TURNED))
         ]
-        larger_low = [keep.tile([P, 2 * T], BF16, name="larger_low%d" % k) for k in range(2)]
-        larger_high = [keep.tile([P, 2 * TURNED], BF16, name="larger_high%d" % k) for k in range(2)]
+        larger01 = [keep.tile([P, 2 * T], BF16, name="larger01_%d" % k) for k in range(2)]
+        larger23 = [keep.tile([P, 2 * TURNED], BF16, name="larger23_%d" % k) for k in range(2)]
         woven_a = keep.tile([P, PACK * HALF], BF16, name="woven_a", align_bytes=64)
-        woven_b = keep.tile([P, PACK * 256], BF16, name="woven_b", align_bytes=64)
+        woven_b = keep.tile([P, PACK * UNIT], BF16, name="woven_b", align_bytes=64)
         woven_rest = keep.tile([P, PACK * REST], BF16, name="woven_rest", align_bytes=64)
+        results = keep.tile([P, HALF], F32, name="results")
+        part_a = slice(0, 2 * HALF)
+        part_b = slice(2 * HALF, 2 * TURNED)
 
-        low_sets = []
+        sets01 = []
         for t in range(2):
-            firsts = fresh("first%d_" % t, T)
-            diffs = fresh("diff%d_" % t, T)
+            firsts = two_tiles("first%d_" % t, T)
+            diffs = two_tiles("diff%d_" % t, T)
             gains = diffs if t == 0 else [h_rows[:, k, :] for k in range(2)]
             for n0 in range(0, T, HALF):
                 cols = slice(n0, n0 + HALF)
                 pairs_with_gains(
                     t, n0, HALF, [x[:, cols] for x in firsts], [x[:, cols] for x in diffs], [x[:, cols] for x in gains]
                 )
-            low_sets.append([(firsts[k], gains[k]) for k in range(2)])
+            sets01.append([(firsts[k], gains[k]) for k in range(2)])
             if t == 0:
-                for u in range(2):
-                    dst, src = weave_views(
-                        h_woven[:, u * 2048 : (u + 1) * 2048], h_rows[:, :, u * HALF : (u + 1) * HALF]
+                for n0 in range(0, T, HALF):
+                    nc.scalar.activation(
+                        h_woven[:, PACK * n0 : PACK * (n0 + HALF)].rearrange("p (c i t) -> p c t i", i=4, t=PACK),
+                        h_rows[:, :, n0 : n0 + HALF].rearrange("p t (c i) -> p c t i", i=4),
+                        ACT.Copy,
                     )
-                    nc.scalar.activation(dst, src, ACT.Copy)
-        nc.vector.quantize_mx(out=h_codes[:].bitcast(FP8X4), scales=h_plane[:], in_=h_woven[:])
-        turned_sums(low_sets, T, [tile[:] for tile in larger_low], 2)
-        reuse = h_woven[:].bitcast(F32)
+        nc.vector.quantize_mx(out=h_codes[:].bitcast(FP8X4), scales=h_scale[:], in_=h_woven[:])
+        turned_sums(sets01, T, [tile[:] for tile in larger01], 4)
+
+        after_h = h_woven[:].bitcast(F32)
         set2a = pairs_with_gains(
             2,
             0,
             HALF,
-            [reuse[:, k * HALF : (k + 1) * HALF] for k in range(2)],
-            fresh("diff2a_", HALF),
-            [low_sets[1][1][k][:, HALF:T] for k in range(2)],
+            [after_h[:, k * HALF : (k + 1) * HALF] for k in range(2)],
+            two_tiles("diff2a_", HALF),
+            [x[:, HALF:T] for x in sets01[1][1]],
         )
-        diff3a = fresh("diff3a_", HALF)
+        diff3a = two_tiles("diff3a_", HALF)
         set3a = pairs_with_gains(
             3,
             0,
             HALF,
-            [reuse[:, (2 + k) * HALF : (3 + k) * HALF] for k in range(2)],
+            [after_h[:, (2 + k) * HALF : (3 + k) * HALF] for k in range(2)],
             diff3a,
-            fresh("gain3a_", HALF),
+            two_tiles("gain3a_", HALF),
         )
-        largest(z_turned[0][:], larger_low[0][:], larger_low[1][:])
-        turned_sums([set2a, set3a], HALF, [tile[:, 0:1024] for tile in larger_high], 2)
-        turn_back(TURNED, woven_rest[:], banks[6], 1)
-        high_b = []
+        largest(z_turned[0][:], larger01[0][:], larger01[1][:])
+        turned_sums([set2a, set3a], HALF, [tile[:, part_a] for tile in larger23], 4)
+        turn_back(TURNED, woven_rest[:], banks[0], 1)
+
+        sets23b = []
         for e in range(2):
-            both = keep.tile([P, HALF], F32, name="diff%db" % (2 + e))
-            halves = [slice(k * 256, (k + 1) * 256) for k in range(2)]
-            firsts = [diff3a[e][:, half] for half in halves]
-            fetch_pairs(2 + e, HALF, 256, firsts, [both[:, half] for half in halves])
+            both = keep.tile([P, 2 * UNIT], F32, name="diff%db" % (2 + e))
+            by_pair = [slice(k * UNIT, (k + 1) * UNIT) for k in range(2)]
+            firsts = [diff3a[e][:, cols] for cols in by_pair]
+            fetch_pairs(2 + e, HALF, UNIT, firsts, [both[:, cols] for cols in by_pair])
             gains = set3a[1][e]
             nc.scalar.activation(gains, both[:], ACT.Relu)
-            high_b.append([(firsts[k], gains[:, halves[k]]) for k in range(2)])
-        largest(z_turned[1][:, 0:1024], larger_high[0][:, 0:1024], larger_high[1][:, 0:1024])
-        turned_sums(high_b, 256, [tile[:, 1024:1536] for tile in larger_high], 7)
+            sets23b.append([(firsts[k], gains[:, by_pair[k]]) for k in range(2)])
+        largest(z_turned[1][:, part_a], larger23[0][:, part_a], larger23[1][:, part_a])
+        turned_sums(sets23b, UNIT, [tile[:, part_b] for tile in larger23], 1)
 
-        space = larger_high[0]
+        four = larger23[0]
         for d in range(LISTS):
-            nc.vector.tensor_copy(space[:, d * REST : (d + 1) * REST], looked_up(2, d, TURNED, REST))
-        pairs = keep.tile([P, 2 * REST], BF16, name="pairs")
-        largest(pairs[:], space[:, 0 : 2 * REST], space[:, 2 * REST : 4 * REST])
-        largest(z_rows[:, 0, :], pairs[:, 0:REST], pairs[:, REST : 2 * REST])
-        largest(z_turned[1][:, 1024:1536], larger_high[0][:, 1024:1536], larger_high[1][:, 1024:1536])
-        for c in range(2):
-            turn_back(256 * c, woven_a[:, 1024 * c : 1024 * (c + 1)], banks[1 + c], 2)
+            nc.vector.tensor_copy(four[:, d * REST : (d + 1) * REST], looked_up(2, d, TURNED, REST))
+        partial = keep.tile([P, 2 * REST], BF16, name="partial")
+        largest(partial[:], four[:, 0 : 2 * REST], four[:, 2 * REST : 4 * REST])
+        largest(z_rows[:, 0, :], partial[:, 0:REST], partial[:, REST : 2 * REST])
+        largest(z_turned[1][:, part_b], larger23[0][:, part_b], larger23[1][:, part_b])
+        for unit in range(2):
+            turn_back(UNIT * unit, woven_a[:, PACK * UNIT * unit : PACK * UNIT * (unit + 1)], banks[3 + unit], 2)
         quantised_a = quantise(0, HALF, woven_a[:])
-        three = [larger_high[0][:, 1024:1280], larger_high[1][:, 1024:1280], woven_a[:, 0:REST]]
+
+        groups = [(0, HALF, banks[6])] + [(HALF + g * P, P, banks[free]) for g, free in enumerate((7, 1, 0, 2))]
+        for g0, width, bank in groups:
+            second_product(0, h_codes[:, g0 : g0 + width], h_scale[:, g0 : g0 + width], bank[:, 0:width])
+
+        three = [larger23[1][:, 0:REST], larger23[1][:, part_b][:, 0:REST], woven_a[:, 0:REST]]
         for d in range(3):
             nc.vector.tensor_copy(three[d], looked_up(3, d, TURNED, REST))
-        largest(pairs[:, 0:REST], three[0], three[1])
-        largest(pairs[:, REST : 2 * REST], pairs[:, 0:REST], three[2])
-        turn_back(HALF, woven_b[:], banks[3], 2)
-        quantised_b = quantise(HALF, 256, woven_b[:])
-        finish(0, HALF, quantised_a, banks[4])
-        finish(HALF, 256, quantised_b, banks[5])
-        for c in range(2):
-            nc.vector.tensor_copy(woven_b[:, c * P : (c + 1) * P], looked_up(3, 3, TURNED + c * P, P))
-        for c in range(2):
-            cols = slice(c * P, (c + 1) * P)
-            largest(z_rows[:, 1, cols], pairs[:, REST + c * P : REST + (c + 1) * P], woven_b[:, cols])
-        for c in range(2):
+        largest(partial[:, 0:REST], three[0], three[1])
+        largest(partial[:, REST : 2 * REST], partial[:, 0:REST], three[2])
+
+        def rest_block(b):
+            return woven_rest[:, b * PACK * P : (b + 1) * PACK * P]
+
+        def last_list(b, fourth):
+            cols = slice(b * P, (b + 1) * P)
+            nc.vector.tensor_copy(fourth, looked_up(3, 3, TURNED + b * P, P))
+            largest(z_rows[:, 1, cols], partial[:, REST + b * P : REST + (b + 1) * P], fourth)
             nc.vector.tensor_copy(
-                woven_rest[:, c * 512 : (c + 1) * 512].rearrange("p (n u e) -> p n u e", u=2, e=2)[:, :, 1, :],
-                z_rows[:, :, c * P : (c + 1) * P].rearrange("p e n -> p n e"),
+                rest_block(b).rearrange("p (n u e) -> p n u e", u=2, e=2)[:, :, 1, :],
+                z_rows[:, :, cols].rearrange("p e n -> p n e"),
             )
-        for c in range(2):
-            n0 = TURNED + c * P
-            finish(n0, P, quantise(n0, P, woven_rest[:, c * 512 : (c + 1) * 512]), banks[6 + c])
+
+        turn_back(HALF, woven_b[:], banks[5], 2)
+        last_list(0, three[0][:, 0:P])
+        quantised_b = quantise(HALF, UNIT, woven_b[:])
+        finish(0, HALF, quantised_a, z_turned[0][:, 2 * HALF : 2 * T].bitcast(F32))
+        finish(HALF, UNIT, quantised_b, results[:, 0:UNIT])
+        last_list(1, woven_b[:, 0:P])
+        for b in range(2):
+            n0 = TURNED + b * P
+            finish(n0, P, quantise(n0, P, rest_block(b)), results[:, n0 - HALF : n0 - HALF + P])

from contextlib import ExitStack

import concourse.mybir as mybir
from concourse.masks import make_identity

K, T, H, N = 512, 1024, 512, 128
FLOPS = 2 * K * H * T + 2 * 2 * H * N * T

F32 = mybir.dt.float32
BF16 = mybir.dt.bfloat16
I32 = mybir.dt.int32
U32 = mybir.dt.uint32
U16 = mybir.dt.uint16
U8 = mybir.dt.uint8
FP8X4 = mybir.dt.float8_e4m3fn_x4
FP4X4 = mybir.dt.float4_e2m1fn_x4
ACT = mybir.ActivationFunctionType
ALU = mybir.AluOpType

P = 128
PACK = 4
LISTS = 4
BANKS = 8
BANK = 512
HALF = T // 2
UNIT = 256
TURNED = HALF + UNIT
REST = T - TURNED


def tile_picked_wsagecat_max_l_kernel(
    tc, x_words, x_scales, w1, w2_words, w2_scales, w3_words, w3_scales, pos1, pos2, pos3, pos4, out
):
    nc = tc.nc
    with ExitStack() as ctx:
        keep = ctx.enter_context(tc.tile_pool(name="keep", bufs=1))
        psum = ctx.enter_context(tc.psum_pool(name="psum", bufs=1))
        banks = [psum.tile([P, BANK], F32, name="bank%d" % number) for number in range(BANKS)]

        lists = [keep.tile([P, T // 16], U16, name="list%d" % d) for d in range(LISTS)]
        x_scale = keep.tile([P, T], U8, name="x_scale", align_bytes=64)
        w23_scale = keep.tile([P, 2 * N], U8, name="w23_scale", align_bytes=64)
        w1_raw = [keep.tile([P, 2, H], F32, name="w1_raw%d" % half) for half in range(2)]
        x_codes = [keep.tile([P, HALF], U32, name="x_codes%d" % half, align_bytes=64) for half in range(2)]
        w23_codes = [keep.tile([P, 2 * N], U8, name="w%d_codes" % w, align_bytes=64) for w in (2, 3)]

        nc.vector.memset(x_scale[:].bitcast(I32), 0)
        nc.vector.memset(w23_scale[:].bitcast(I32), 0)
        w1_rows = w1.rearrange("(p j) c -> p j c", j=PACK)
        x_flat = x_words[0].rearrange("p n t -> p (n t)").bitcast(I32)
        for half in range(2):
            nc.sync.dma_start(w1_raw[half][:], w1_rows[:, 2 * half : 2 * half + 2, :])
        for q in range(4):
            nc.sync.dma_start(
                x_scale[32 * q : 32 * q + 4, :].bitcast(I32), x_scales[0][4 * q : 4 * q + 4, :].bitcast(I32)
            )
        for half in range(2):
            nc.sync.dma_start(x_codes[half][:].bitcast(I32), x_flat[:, half * HALF : (half + 1) * HALF])
        for tile, pos in zip(lists, (pos1, pos2, pos3, pos4)):
            nc.sync.dma_start(tile[:], pos)
        for which, (words, scales) in enumerate(((w2_words, w2_scales), (w3_words, w3_scales))):
            nc.sync.dma_start(w23_codes[which][:].bitcast(I32), words[0].bitcast(I32))
            for q in range(4):
                nc.sync.dma_start(
                    w23_scale[32 * q : 32 * q + 4, which * N : (which + 1) * N].bitcast(I32),
                    scales[0][4 * q : 4 * q + 4, :].bitcast(I32),
                )

        w_first = keep.tile([P, P * PACK], BF16, name="w_first", align_bytes=64)
        w_others = keep.tile([P, PACK - 1, P * PACK], BF16, name="w_others", align_bytes=64)
        w_codes0 = keep.tile([P, P], U32, name="w_codes0", align_bytes=64)
        w_scale0 = keep.tile([P, P], U8, name="w_scale0", align_bytes=64)
        w_codes1 = keep.tile([P, P], U32, name="w_codes1", align_bytes=64)
        w_scale1 = keep.tile([P, P], U8, name="w_scale1", align_bytes=64)
        w_codes23 = keep.tile([P, 2 * P], U32, name="w_codes23", align_bytes=64)
        w_scale23 = keep.tile([P, 2 * P], U8, name="w_scale23", align_bytes=64)
        for half in range(2):
            dealt = w1_raw[half][:].rearrange("p j (m t) -> p m j t", t=PACK)
            rows = slice(2 * half, 2 * half + 2)
            nc.vector.tensor_copy(w_first[:].rearrange("p (m j) -> p m j", j=PACK)[:, :, rows], dealt[:, :, :, 0])
            nc.scalar.activation(
                w_others[:].rearrange("p t (m j) -> p m j t", j=PACK)[:, :, rows, :],
                dealt[:, :, :, 1:PACK],
                ACT.Copy,
            )
        nc.vector.quantize_mx(out=w_codes0[:].bitcast(FP8X4), scales=w_scale0[:], in_=w_first[:])
        nc.vector.quantize_mx(out=w_codes1[:].bitcast(FP8X4), scales=w_scale1[:], in_=w_others[:, 0, :])
        nc.vector.quantize_mx(
            out=w_codes23[:].bitcast(FP8X4),
            scales=w_scale23[:],
            in_=w_others[:, 1:3, :].rearrange("p t c -> p (t c)"),
        )
        stationary = [
            (w_codes0[:], w_scale0[:]),
            (w_codes1[:], w_scale1[:]),
            (w_codes23[:, 0:P], w_scale23[:, 0:P]),
            (w_codes23[:, P : 2 * P], w_scale23[:, P : 2 * P]),
        ]

        ident = keep.tile([P, P], F32, name="ident")
        make_identity(nc, ident[:])
        h = [keep.tile([P, T], F32, name="h%d" % t) for t in range(PACK)]
        h_rows = keep.tile([P, PACK, T], F32, name="h_rows")
        for t in range(PACK):
            width = T // 4 if t == 0 else HALF
            for piece, n0 in enumerate(range(0, T, width)):
                acc = banks[piece if t == 0 else 2 + piece][:, 0:width]
                half, c0 = divmod(n0, HALF)
                nc.tensor.matmul_mx(
                    out=acc,
                    lhsT=stationary[t][0].bitcast(FP8X4),
                    lhsT_scale=stationary[t][1],
                    rhs=x_codes[half][:, c0 : c0 + width].bitcast(FP8X4),
                    rhs_scale=x_scale[:, n0 : n0 + width],
                    start=True,
                    stop=True,
                )
                if t == 0 and n0 + width == T:
                    nc.vector.tensor_scalar_max(h[t][:, n0 : n0 + width], acc, 0.0)
                else:
                    nc.scalar.activation(h[t][:, n0 : n0 + width], acc, ACT.Relu)
            nc.sync.dma_start(h_rows[:, t, :], h[t][:])

        h_woven = keep.tile([P, PACK * T], BF16, name="h_woven", align_bytes=64)
        h_codes = keep.tile([P, T], U32, name="h_codes", align_bytes=64)
        h_scale = keep.tile([P, T], U8, name="h_scale", align_bytes=64)

        def looked_up(t, d, n0, n):
            return h[t][:].indirect(lists[d][:, n0 // 16 : (n0 + n) // 16])

        def fetch_pairs(t, n0, n, firsts, diffs):
            for k in range(2):
                nc.vector.tensor_copy(firsts[k], looked_up(t, 2 * k, n0, n))
            for k in range(2):
                nc.vector.tensor_tensor(diffs[k], looked_up(t, 2 * k + 1, n0, n), firsts[k], ALU.subtract)

        def pairs_with_gains(t, n0, n, firsts, diffs, gains):
            fetch_pairs(t, n0, n, firsts, diffs)
            for k in range(2):
                nc.scalar.activation(gains[k], diffs[k], ACT.Relu)
            return [(firsts[k], gains[k]) for k in range(2)]

        def two_tiles(label, n):
            return [keep.tile([P, n], F32, name="%s%d" % (label, k))[:] for k in range(2)]

        def turned_sums(sets, n, larger, first_bank):
            for k in range(2):
                for c0 in range(0, n, UNIT):
                    bank = banks[(first_bank + (k * n + c0) // UNIT) % BANKS]
                    for e in range(2):
                        for b in range(2):
                            cols = slice(c0 + b * P, c0 + (b + 1) * P)
                            spot = bank[:, (2 * b + e) * P : (2 * b + e + 1) * P]
                            first, gain = sets[e][k]
                            nc.tensor.matmul(spot, first[:, cols], ident[:], start=True, stop=False, is_transpose=True)
                            nc.tensor.matmul(spot, gain[:, cols], ident[:], start=False, stop=True, is_transpose=True)
                    nc.scalar.copy(
                        larger[k][:, 2 * c0 : 2 * (c0 + UNIT)].rearrange("q (b p e) -> q b p e", b=2, e=2),
                        bank[:].rearrange("q (b e p) -> q b p e", b=2, e=2),
                    )

        def turn_back(n0, woven, bank, pairs_of_sets):
            for b in range(2):
                for u in range(pairs_of_sets):
                    col = n0 + b * P
                    nc.tensor.transpose(
                        bank[:, (2 * b + u) * P : (2 * b + u + 1) * P],
                        z_turned[u][:, 2 * col : 2 * (col + P)].bitcast(F32),
                        ident[:],
                    )
            nc.scalar.copy(
                woven.bitcast(F32).rearrange("p (b n u) -> p b n u", b=2, u=2)[:, :, :, 0:pairs_of_sets],
                bank[:].rearrange("p (b u n) -> p b n u", b=2, u=2)[:, :, :, 0:pairs_of_sets],
            )

        def quantise(n0, n, woven):
            z_codes = keep.tile([P, n], U32, name="z_codes%d" % n0, align_bytes=64)
            z_scale = keep.tile([P, n], U8, name="z_scale%d" % n0, align_bytes=64)
            nc.vector.quantize_mx(out=z_codes[:].bitcast(FP8X4), scales=z_scale[:], in_=woven)
            return z_codes, z_scale

        def second_product(which, codes, scale, total):
            nc.tensor.matmul_mx(
                out=total,
                lhsT=w23_codes[which][:].bitcast(FP4X4),
                lhsT_scale=w23_scale[:, which * N : (which + 1) * N],
                rhs=codes.bitcast(FP8X4),
                rhs_scale=scale,
                start=(which == 0),
                stop=(which == 1),
            )

        def finish(n0, n, quantised, result):
            z_codes, z_scale = quantised
            for g0, width, bank in groups:
                if n0 <= g0 < n0 + n:
                    cols = slice(g0 - n0, g0 - n0 + width)
                    second_product(1, z_codes[:, cols], z_scale[:, cols], bank[:, 0:width])
                    if g0 + width == T:
                        nc.vector.tensor_copy(result[:, cols], bank[:, 0:width])
                    else:
                        nc.scalar.copy(result[:, cols], bank[:, 0:width])
            nc.sync.dma_start(out[:, n0 : n0 + n], result)

        def largest(dst, one, other):
            nc.vector.tensor_tensor(dst, one, other, ALU.max)

        z_rows = keep.tile([P, 2, REST], BF16, name="z_rows")
        z_turned = [
            keep.tile([P, 2 * n], BF16, name="z_turned%d" % u, align_bytes=64) for u, n in enumerate((T, TURNED))
        ]
        larger01 = [keep.tile([P, 2 * T], BF16, name="larger01_%d" % k) for k in range(2)]
        larger23 = [keep.tile([P, 2 * TURNED], BF16, name="larger23_%d" % k) for k in range(2)]
        woven_a = keep.tile([P, PACK * HALF], BF16, name="woven_a", align_bytes=64)
        woven_b = keep.tile([P, PACK * UNIT], BF16, name="woven_b", align_bytes=64)
        woven_rest = keep.tile([P, PACK * REST], BF16, name="woven_rest", align_bytes=64)
        results = keep.tile([P, HALF], F32, name="results")
        part_a = slice(0, 2 * HALF)
        part_b = slice(2 * HALF, 2 * TURNED)

        sets01 = []
        for t in range(2):
            firsts = two_tiles("first%d_" % t, T)
            diffs = two_tiles("diff%d_" % t, T)
            gains = diffs if t == 0 else [h_rows[:, k, :] for k in range(2)]
            for n0 in range(0, T, HALF):
                cols = slice(n0, n0 + HALF)
                pairs_with_gains(
                    t, n0, HALF, [x[:, cols] for x in firsts], [x[:, cols] for x in diffs], [x[:, cols] for x in gains]
                )
            sets01.append([(firsts[k], gains[k]) for k in range(2)])
            if t == 0:
                for n0 in range(0, T, HALF):
                    nc.scalar.activation(
                        h_woven[:, PACK * n0 : PACK * (n0 + HALF)].rearrange("p (c i t) -> p c t i", i=4, t=PACK),
                        h_rows[:, :, n0 : n0 + HALF].rearrange("p t (c i) -> p c t i", i=4),
                        ACT.Copy,
                    )
        nc.vector.quantize_mx(out=h_codes[:].bitcast(FP8X4), scales=h_scale[:], in_=h_woven[:])
        turned_sums(sets01, T, [tile[:] for tile in larger01], 4)

        after_h = h_woven[:].bitcast(F32)
        set2a = pairs_with_gains(
            2,
            0,
            HALF,
            [after_h[:, k * HALF : (k + 1) * HALF] for k in range(2)],
            two_tiles("diff2a_", HALF),
            [x[:, HALF:T] for x in sets01[1][1]],
        )
        diff3a = two_tiles("diff3a_", HALF)
        set3a = pairs_with_gains(
            3,
            0,
            HALF,
            [after_h[:, (2 + k) * HALF : (3 + k) * HALF] for k in range(2)],
            diff3a,
            two_tiles("gain3a_", HALF),
        )
        largest(z_turned[0][:], larger01[0][:], larger01[1][:])
        turned_sums([set2a, set3a], HALF, [tile[:, part_a] for tile in larger23], 4)
        turn_back(TURNED, woven_rest[:], banks[0], 1)

        sets23b = []
        for e in range(2):
            both = keep.tile([P, 2 * UNIT], F32, name="diff%db" % (2 + e))
            by_pair = [slice(k * UNIT, (k + 1) * UNIT) for k in range(2)]
            firsts = [diff3a[e][:, cols] for cols in by_pair]
            fetch_pairs(2 + e, HALF, UNIT, firsts, [both[:, cols] for cols in by_pair])
            gains = set3a[1][e]
            nc.scalar.activation(gains, both[:], ACT.Relu)
            sets23b.append([(firsts[k], gains[:, by_pair[k]]) for k in range(2)])
        largest(z_turned[1][:, part_a], larger23[0][:, part_a], larger23[1][:, part_a])
        turned_sums(sets23b, UNIT, [tile[:, part_b] for tile in larger23], 1)

        four = larger23[0]
        for d in range(LISTS):
            nc.vector.tensor_copy(four[:, d * REST : (d + 1) * REST], looked_up(2, d, TURNED, REST))
        partial = keep.tile([P, 2 * REST], BF16, name="partial")
        largest(partial[:], four[:, 0 : 2 * REST], four[:, 2 * REST : 4 * REST])
        largest(z_rows[:, 0, :], partial[:, 0:REST], partial[:, REST : 2 * REST])
        largest(z_turned[1][:, part_b], larger23[0][:, part_b], larger23[1][:, part_b])
        for unit in range(2):
            turn_back(UNIT * unit, woven_a[:, PACK * UNIT * unit : PACK * UNIT * (unit + 1)], banks[3 + unit], 2)
        quantised_a = quantise(0, HALF, woven_a[:])

        groups = [(0, HALF, banks[6])] + [(HALF + g * P, P, banks[free]) for g, free in enumerate((7, 1, 0, 2))]
        for g0, width, bank in groups:
            second_product(0, h_codes[:, g0 : g0 + width], h_scale[:, g0 : g0 + width], bank[:, 0:width])

        three = [larger23[1][:, 0:REST], larger23[1][:, part_b][:, 0:REST], woven_a[:, 0:REST]]
        for d in range(3):
            nc.vector.tensor_copy(three[d], looked_up(3, d, TURNED, REST))
        largest(partial[:, 0:REST], three[0], three[1])
        largest(partial[:, REST : 2 * REST], partial[:, 0:REST], three[2])

        def rest_block(b):
            return woven_rest[:, b * PACK * P : (b + 1) * PACK * P]

        def last_list(b, fourth):
            cols = slice(b * P, (b + 1) * P)
            nc.vector.tensor_copy(fourth, looked_up(3, 3, TURNED + b * P, P))
            largest(z_rows[:, 1, cols], partial[:, REST + b * P : REST + (b + 1) * P], fourth)
            nc.vector.tensor_copy(
                rest_block(b).rearrange("p (n u e) -> p n u e", u=2, e=2)[:, :, 1, :],
                z_rows[:, :, cols].rearrange("p e n -> p n e"),
            )

        turn_back(HALF, woven_b[:], banks[5], 2)
        last_list(0, three[0][:, 0:P])
        quantised_b = quantise(HALF, UNIT, woven_b[:])
        finish(0, HALF, quantised_a, z_turned[0][:, 2 * HALF : 2 * T].bitcast(F32))
        finish(HALF, UNIT, quantised_b, results[:, 0:UNIT])
        last_list(1, woven_b[:, 0:P])
        for b in range(2):
            n0 = TURNED + b * P
            finish(n0, P, quantise(n0, P, rest_block(b)), results[:, n0 - HALF : n0 - HALF + P])
